import numpy as np
import ml_dtypes

BF16 = ml_dtypes.bfloat16


def bf(x):
    return np.asarray(x, np.float32).astype(BF16)


def f32(x):
    return np.asarray(x, np.float32)


def f64(x):
    return np.asarray(x).astype(np.float64)


def striped(idx):
    return np.tile(idx.reshape(-1, 16).T, (8, 1))


def rows(idx, k):
    return np.tile(idx, (k, 1))


def look(tab, idx):
    return np.take_along_axis(f64(tab), rows(idx, len(tab)), axis=1)


K, S, V, N, M = 256, 256, 64, 64, 256


def setup_inputs():
    return {"tab": f32(np.random.standard_normal((K, S))), "w": bf(np.random.standard_normal((K, M)) / np.sqrt(K)), "b": f32(0.5 * np.random.standard_normal((M, 1))), "offs": striped(np.random.randint(0, S, N))}


def reference(tab, w, b, offs):
    idx = offs[:16].T.reshape(-1)
    t = look(tab, idx)
    x = (t - 0.125) * 1.5
    y = f64(w).T @ x
    return np.maximum(y + f64(b), 0.0)

@@ -1,0 +1,59 @@
+import concourse.mybir as mybir
+
+F32 = mybir.dt.float32
+BF16 = mybir.dt.bfloat16
+U16 = mybir.dt.uint16
+ADD = mybir.AluOpType.add
+MULT = mybir.AluOpType.mult
+MAX = mybir.AluOpType.max
+
+P = 128
+ROWS = 256
+COLS = 256
+LIST = 64
+OUTS = 256
+SHIFT = 0.125
+SCALE = 1.5
+FLOPS = 2 * ROWS * OUTS * LIST
+
+
+def tile_lookup_deq_nrm_relu_kernel(tc, tab, w, b, offs, out):
+    nc = tc.nc
+    row_blocks = ROWS // P
+    out_blocks = OUTS // P
+    with (
+        tc.tile_pool(name="held", bufs=1) as held,
+        tc.psum_pool(name="psum", bufs=1) as psum,
+    ):
+        offsets = held.tile([P, LIST // 16], U16, name="offsets")
+        nc.sync.dma_start(offsets[:], offs)
+
+        windows = [held.tile([P, COLS], F32, name=f"window{k}") for k in range(row_blocks)]
+        weights = [held.tile([P, OUTS], BF16, name=f"weights{k}") for k in range(row_blocks)]
+        biases = [held.tile([P, 1], F32, name=f"bias{h}") for h in range(out_blocks)]
+        nc.scalar.dma_start(windows[0][:], tab[0:P, :])
+        nc.sync.dma_start(windows[1][:], tab[P : 2 * P, :])
+        for k in range(row_blocks):
+            nc.scalar.dma_start(weights[k][:], w[k * P : (k + 1) * P, :])
+        for h in range(out_blocks):
+            nc.sync.dma_start(biases[h][:], b[h * P : (h + 1) * P, :])
+
+        xs = [held.tile([P, LIST], BF16, name=f"x{k}") for k in range(row_blocks)]
+        for k in range(row_blocks):
+            nc.vector.tensor_scalar(
+                xs[k][:], windows[k][:].indirect(offsets[:]), SCALE, -SHIFT * SCALE, MULT, ADD
+            )
+
+        for h in range(out_blocks):
+            y = psum.tile([P, LIST], F32, name=f"y{h}")
+            for k in range(row_blocks):
+                nc.tensor.matmul(
+                    y[:],
+                    weights[k][:, h * P : (h + 1) * P],
+                    xs[k][:],
+                    start=k == 0,
+                    stop=k == row_blocks - 1,
+                )
+            result = held.tile([P, LIST], F32, name=f"result{h}")
+            nc.vector.tensor_scalar(result[:], y[:], biases[h][:], 0.0, ADD, MAX)
+            nc.sync.dma_start(out[h * P : (h + 1) * P, :], result[:])

@@ -28,15 +28,14 @@ def tile_lookup_deq_nrm_relu_kernel(tc, tab, w, b, offs, out):
         offsets = held.tile([P, LIST // 16], U16, name="offsets")
         nc.sync.dma_start(offsets[:], offs)
 
+        tab_rows = tab.rearrange("(p k) c -> p k c", k=row_blocks)
         windows = [held.tile([P, COLS], F32, name=f"window{k}") for k in range(row_blocks)]
-        weights = [held.tile([P, OUTS], BF16, name=f"weights{k}") for k in range(row_blocks)]
-        biases = [held.tile([P, 1], F32, name=f"bias{h}") for h in range(out_blocks)]
-        nc.scalar.dma_start(windows[0][:], tab[0:P, :])
-        nc.sync.dma_start(windows[1][:], tab[P : 2 * P, :])
-        for k in range(row_blocks):
-            nc.scalar.dma_start(weights[k][:], w[k * P : (k + 1) * P, :])
-        for h in range(out_blocks):
-            nc.sync.dma_start(biases[h][:], b[h * P : (h + 1) * P, :])
+        weights = held.tile([P, row_blocks, OUTS], BF16, name="weights")
+        bias = held.tile([P, out_blocks], F32, name="bias")
+        nc.scalar.dma_start(windows[0][:], tab_rows[:, 0, :])
+        nc.sync.dma_start(windows[1][:], tab_rows[:, 1, :])
+        nc.scalar.dma_start(weights[:], w.rearrange("(p k) m -> p k m", k=row_blocks))
+        nc.sync.dma_start(bias[:], b.rearrange("(p h) one -> p (h one)", h=out_blocks))
 
         xs = [held.tile([P, LIST], BF16, name=f"x{k}") for k in range(row_blocks)]
         for k in range(row_blocks):
@@ -44,16 +43,16 @@ def tile_lookup_deq_nrm_relu_kernel(tc, tab, w, b, offs, out):
                 xs[k][:], windows[k][:].indirect(offsets[:]), SCALE, -SHIFT * SCALE, MULT, ADD
             )
 
+        result = held.tile([P, out_blocks, LIST], F32, name="result")
         for h in range(out_blocks):
             y = psum.tile([P, LIST], F32, name=f"y{h}")
             for k in range(row_blocks):
                 nc.tensor.matmul(
                     y[:],
-                    weights[k][:, h * P : (h + 1) * P],
+                    weights[:, k, h::out_blocks],
                     xs[k][:],
                     start=k == 0,
                     stop=k == row_blocks - 1,
                 )
-            result = held.tile([P, LIST], F32, name=f"result{h}")
-            nc.vector.tensor_scalar(result[:], y[:], biases[h][:], 0.0, ADD, MAX)
-            nc.sync.dma_start(out[h * P : (h + 1) * P, :], result[:])
+            nc.vector.tensor_scalar(result[:, h, :], y[:], bias[:, h : h + 1], 0.0, ADD, MAX)
+        nc.sync.dma_start(out.rearrange("(p h) j -> p h j", h=out_blocks), result[:])

@@ -43,16 +43,18 @@ def tile_lookup_deq_nrm_relu_kernel(tc, tab, w, b, offs, out):
                 xs[k][:], windows[k][:].indirect(offsets[:]), SCALE, -SHIFT * SCALE, MULT, ADD
             )
 
-        result = held.tile([P, out_blocks, LIST], F32, name="result")
-        for h in range(out_blocks):
-            y = psum.tile([P, LIST], F32, name=f"y{h}")
-            for k in range(row_blocks):
+        ys = [psum.tile([P, LIST], F32, name=f"y{h}") for h in range(out_blocks)]
+        for k in range(row_blocks):
+            for h in range(out_blocks):
                 nc.tensor.matmul(
-                    y[:],
+                    ys[h][:],
                     weights[:, k, h::out_blocks],
                     xs[k][:],
                     start=k == 0,
                     stop=k == row_blocks - 1,
                 )
-            nc.vector.tensor_scalar(result[:, h, :], y[:], bias[:, h : h + 1], 0.0, ADD, MAX)
+
+        result = held.tile([P, out_blocks, LIST], F32, name="result")
+        for h in range(out_blocks):
+            nc.vector.tensor_scalar(result[:, h, :], ys[h][:], bias[:, h : h + 1], 0.0, ADD, MAX)
         nc.sync.dma_start(out.rearrange("(p h) j -> p h j", h=out_blocks), result[:])

import concourse.mybir as mybir

F32 = mybir.dt.float32
BF16 = mybir.dt.bfloat16
U16 = mybir.dt.uint16
ADD = mybir.AluOpType.add
MULT = mybir.AluOpType.mult
MAX = mybir.AluOpType.max

P = 128
ROWS = 256
COLS = 256
LIST = 64
OUTS = 256
SHIFT = 0.125
SCALE = 1.5
FLOPS = 2 * ROWS * OUTS * LIST


def tile_lookup_deq_nrm_relu_kernel(tc, tab, w, b, offs, out):
    nc = tc.nc
    row_blocks = ROWS // P
    out_blocks = OUTS // P
    with (
        tc.tile_pool(name="held", bufs=1) as held,
        tc.psum_pool(name="psum", bufs=1) as psum,
    ):
        offsets = held.tile([P, LIST // 16], U16, name="offsets")
        nc.sync.dma_start(offsets[:], offs)

        tab_rows = tab.rearrange("(p k) c -> p k c", k=row_blocks)
        windows = [held.tile([P, COLS], F32, name=f"window{k}") for k in range(row_blocks)]
        weights = held.tile([P, row_blocks, OUTS], BF16, name="weights")
        bias = held.tile([P, out_blocks], F32, name="bias")
        nc.scalar.dma_start(windows[0][:], tab_rows[:, 0, :])
        nc.sync.dma_start(windows[1][:], tab_rows[:, 1, :])
        nc.scalar.dma_start(weights[:], w.rearrange("(p k) m -> p k m", k=row_blocks))
        nc.sync.dma_start(bias[:], b.rearrange("(p h) one -> p (h one)", h=out_blocks))

        xs = [held.tile([P, LIST], BF16, name=f"x{k}") for k in range(row_blocks)]
        for k in range(row_blocks):
            nc.vector.tensor_scalar(
                xs[k][:], windows[k][:].indirect(offsets[:]), SCALE, -SHIFT * SCALE, MULT, ADD
            )

        ys = [psum.tile([P, LIST], F32, name=f"y{h}") for h in range(out_blocks)]
        for k in range(row_blocks):
            for h in range(out_blocks):
                nc.tensor.matmul(
                    ys[h][:],
                    weights[:, k, h::out_blocks],
                    xs[k][:],
                    start=k == 0,
                    stop=k == row_blocks - 1,
                )

        result = held.tile([P, out_blocks, LIST], F32, name="result")
        for h in range(out_blocks):
            nc.vector.tensor_scalar(result[:, h, :], ys[h][:], bias[:, h : h + 1], 0.0, ADD, MAX)
        nc.sync.dma_start(out.rearrange("(p h) j -> p h j", h=out_blocks), result[:])
